import numpy as np
import ml_dtypes


def mxq(x, axis, fmt="e4m3"):
    dtype, down = {"e4m3": (ml_dtypes.float8_e4m3fn, 7), "e5m2": (ml_dtypes.float8_e5m2, 14)}[fmt]
    v = np.moveaxis(np.asarray(x, np.float32).astype(ml_dtypes.bfloat16).astype(np.float64), axis, -1)
    blocks = v.reshape(v.shape[:-1] + (-1, 32))
    amax = np.abs(blocks).max(-1, keepdims=True)
    byte = np.maximum(np.where(amax > 0, np.frexp(amax)[1] - 1 + 127, 0) - down, 1)
    scale = np.exp2(byte - 127.0)
    codes = (blocks / scale).astype(np.float32).astype(dtype).astype(np.float64)
    return np.moveaxis((codes * scale).reshape(v.shape), -1, axis)


WIDE = False


def mx_kscale(k):
    if not WIDE:
        return np.ones(k)
    levels = np.array([10, -10, 5, -5, 0])
    if k % 512:
        return np.exp2(np.random.permutation(np.resize(levels, k // 32))).repeat(32)
    a = np.empty((k // 512, 16))
    for p in range(k // 512):
        a[p, :8] = np.random.permutation(np.resize(levels, 8))
        for g in range(8):
            far = levels[np.abs(levels - a[p, g]) >= 10]
            a[p, g + 8] = far[np.random.randint(len(far))]
    return np.exp2(a.ravel()).repeat(32)


def f64(x):
    return np.asarray(x).astype(np.float64)


def striped(idx):
    return np.tile(idx.reshape(-1, 16).T, (8, 1)).astype(np.uint16)


def unstriped(offs):
    return offs[:16].T.reshape(-1).astype(np.int64)


def striped8(idx):
    return np.concatenate([x.reshape(-1, 16).T for x in idx]).astype(np.uint16)


def runs(offs, k):
    lists = np.stack([offs[16 * r : 16 * r + 16].T.reshape(-1) for r in range(8)]).astype(np.int64)
    return lists[np.arange(k) % 512 // 64]


def pack_weight(w):
    k, n = w.shape
    w = f64(np.asarray(w, np.float32).astype(ml_dtypes.bfloat16)).reshape(k // 32, 32, n)
    amax = np.abs(w).max(1)
    byte = np.clip(np.where(amax > 0, np.frexp(amax)[1] - 1 + 127 - 7, 1), 1, 254)
    scaled = (w * np.exp2(127.0 - byte)[:, None, :]).reshape(k, n).astype(np.float32)
    words = np.ascontiguousarray(scaled.reshape(k // 512, 128, 4, n).transpose(0, 1, 3, 2)).astype(ml_dtypes.float8_e4m3fn).view(np.uint8)
    return words, np.ascontiguousarray(byte.astype(np.uint8).reshape(k // 512, 16, n))


def unpack_weight(words, scales):
    g, p, n, _ = words.shape
    vals = np.ascontiguousarray(words).view(ml_dtypes.float8_e4m3fn).astype(np.float64) * np.repeat(np.exp2(scales.astype(np.float64) - 127.0), 8, axis=1)[..., None]
    return vals.transpose(0, 1, 3, 2).reshape(g * 512, n)


def relu(v):
    return np.maximum(v, 0.0)

def planes(y):
    n, m = y.shape
    v = y.astype(np.float32).astype(ml_dtypes.bfloat16).astype(np.float64).reshape(n // 32, 32, m)
    top = np.abs(v).max(1)
    byte = np.clip(np.where(top > 0, np.frexp(top)[1] - 1 + 127 - 7, 1), 1, 254)
    codes = (v * np.exp2(127.0 - byte)[:, None, :]).reshape(n, m).astype(np.float32).astype(ml_dtypes.float8_e4m3fn).view(np.uint8)
    words = codes.reshape(n // 512, 128, 4, m).transpose(0, 1, 3, 2)
    return np.ascontiguousarray(words), np.ascontiguousarray(byte.astype(np.uint8).reshape(n // 512, 16, m))


K, T, S, G, H, C = 512, 1024, 512, 2048, 512, 512


def setup_inputs():
    n = np.random.standard_normal
    s = mx_kscale(K)[:, None]
    packed_xT = pack_weight(n((K, T)) * s)
    packed_dT = pack_weight(n((K, G)) / s)
    return {
        "x_words": packed_xT[0],
        "x_scales": packed_xT[1],
        "d_words": packed_dT[0],
        "d_scales": packed_dT[1],
        "gs": (np.random.uniform(0.5, 1.5, (K, 1)) / s).astype(np.float32),
        "offs": striped(np.random.permutation(T)[:S]),
        "k1": striped8(np.random.randint(0, G, (8, H))),
        "n1": striped8(np.stack([np.random.permutation(S) for _ in range(8)])),
        "n2": striped8(np.stack([np.random.permutation(S) for _ in range(8)])),
        "cand": striped(np.random.permutation(T)[:C]),
        "n3": striped8(np.stack([np.random.permutation(S) for _ in range(8)])),
        "n4": striped8(np.stack([np.random.permutation(S) for _ in range(8)])),
    }


def reference(x_words, x_scales, d_words, d_scales, gs, offs, k1, n1, n2, cand, n3, n4):
    x_cand = unpack_weight(x_words, x_scales)[:, unstriped(cand)]
    d_k1 = unpack_weight(d_words, d_scales)[np.arange(K)[:, None], runs(k1, K)]
    xq = unpack_weight(x_words, x_scales)[:, unstriped(offs)]
    h = 0.0625 * (d_k1.T @ xq)
    pa = h - (h[np.arange(H)[:, None], runs(n1, H)])
    pb = h[np.arange(H)[:, None], runs(n2, H)] - h
    z = f64(gs) * (relu(np.minimum(pa, pb)) - (relu(-1.0 * np.maximum(pa, pb))))
    s = 0.0625 * ((x_cand.T @ mxq(z, 0, "e4m3")))
    out_0 = 0.75 * (s[np.arange(C)[:, None], runs(n3, C)] + s[np.arange(C)[:, None], runs(n4, C)]) - s
    return (out_0,) + planes(out_0)

@@ -1,0 +1,226 @@
+from contextlib import ExitStack
+
+import concourse.mybir as mybir
+
+K, T, S, G = 512, 1024, 512, 2048
+FLOPS = 2 * 2 * 512 * 512 * 512
+
+F32 = mybir.dt.float32
+BF16 = mybir.dt.bfloat16
+I32 = mybir.dt.int32
+U32 = mybir.dt.uint32
+U16 = mybir.dt.uint16
+U8 = mybir.dt.uint8
+FP8X4 = mybir.dt.float8_e4m3fn_x4
+ALU = mybir.AluOpType
+ACT = mybir.ActivationFunctionType
+
+P = 128
+PACK = 4
+CH1 = [(0, 256), (256, 128), (384, 128)]
+CH2 = [(0, 256), (256, 128), (384, 128)]
+
+
+def tile_picked_pqcminmodlap_none_po_kernel(
+    tc, x_words, x_scales, d_words, d_scales, gs, offs, k1, n1, n2, cand, n3, n4, out_0, out_1, out_2
+):
+    nc = tc.nc
+    with ExitStack() as ctx:
+        keep = ctx.enter_context(tc.tile_pool(name="keep", bufs=1))
+        psum = ctx.enter_context(tc.psum_pool(name="psum", bufs=1))
+
+        def sb(name, shape, dtype):
+            return keep.tile(shape, dtype, name=name, align_bytes=64)
+
+        def load_list(name, src):
+            tile = sb(name, [P, S // 16], U16)
+            nc.sync.dma_start(tile[:], src)
+            return tile
+
+        def entries(tile, start, count):
+            return tile[:, start // 16 : (start + count) // 16]
+
+        d_bytes = sb("d_bytes", [P, G], U8)
+        x_bytes = sb("x_bytes", [P, T], U8)
+        d_plane = sb("d_plane", [P, S], U8)
+        x_table = sb("x_table", [P, T], U32)
+        d_table = sb("d_table", [P, G], U32)
+        gain = sb("gain", [P, PACK], F32)
+        nc.vector.memset(d_bytes[:].bitcast(I32), 0)
+        nc.gpsimd.memset(x_bytes[:].bitcast(I32), 0)
+        nc.gpsimd.memset(d_plane[:].bitcast(I32), 0)
+
+        k1_t = load_list("k1_t", k1)
+        nc.sync.dma_start(d_bytes[0:P:8, :].bitcast(I32), d_scales[0].bitcast(I32))
+        offs_t = load_list("offs_t", offs)
+        for q in range(4):
+            nc.sync.dma_start(x_bytes[32 * q : 32 * q + 4, :].bitcast(I32), x_scales[0, 4 * q : 4 * q + 4, :].bitcast(I32))
+        nc.sync.dma_start(x_table[:].bitcast(I32), x_words[0].rearrange("p n t -> p (n t)").bitcast(I32))
+        nc.sync.dma_start(d_table[:].bitcast(I32), d_words[0].rearrange("p n t -> p (n t)").bitcast(I32))
+        nc.gpsimd.dma_start(gain[:], gs.rearrange("(p t) o -> p (t o)", t=PACK))
+
+        gain_pos = sb("gain_pos", [P, PACK], F32)
+        gain_neg = sb("gain_neg", [P, PACK], F32)
+        nc.scalar.activation(gain_pos[:], gain[:], ACT.Copy, scale=0.0625)
+        nc.scalar.activation(gain_neg[:], gain[:], ACT.Copy, scale=-0.0625)
+
+        def gather(name, table, lst, dtype):
+            picked = sb(name, [P, S], dtype)
+            nc.vector.tensor_copy(picked[:], table[:].indirect(lst[:]))
+            return picked
+
+        def deal_words(name, picked):
+            dealt = sb(name, [P, S], U32)
+            nc.vector.tensor_copy(
+                dealt[:].rearrange("p (t c i) -> p c t i", t=PACK, i=4),
+                picked[:].rearrange("p (c i t) -> p c t i", t=PACK, i=4),
+            )
+            return dealt
+
+        def deal_bytes(name, picked):
+            dealt = sb(name, [P, S], U8)
+            nc.vector.tensor_copy(
+                dealt[:].rearrange("p (t m) -> p t m", t=PACK),
+                picked[:].rearrange("p (m t) -> p t m", t=PACK),
+            )
+            return dealt
+
+        d_bytes_picked = gather("d_bytes_picked", d_bytes, k1_t, U8)
+        d_bytes_dealt = deal_bytes("d_bytes_dealt", d_bytes_picked)
+        for j in range(4):
+            nc.sync.dma_start(d_plane[j:P:32, :].bitcast(I32), d_bytes_dealt[8 * j : P : 32, :].bitcast(I32))
+        cand_t = load_list("cand_t", cand)
+        n1_t = load_list("n1_t", n1)
+        n2_t = load_list("n2_t", n2)
+        n3_t = load_list("n3_t", n3)
+        n4_t = load_list("n4_t", n4)
+        tok_plane = gather("tok_plane", x_bytes, offs_t, U8)
+        tok_codes = gather("tok_codes", x_table, offs_t, U32)
+        d_picked = gather("d_picked", d_table, k1_t, U32)
+        d_codes = deal_words("d_codes", d_picked)
+
+        pos, neg, h_acc = [], [], []
+        for t in range(PACK):
+            cols = slice(P * t, P * (t + 1))
+            acc = psum.tile([P, S], F32, name=f"h_acc{t}")
+            h_acc.append(acc)
+            nc.tensor.matmul_mx(
+                out=acc[:], lhsT=d_codes[:, cols].bitcast(FP8X4), lhsT_scale=d_plane[:, cols],
+                rhs=tok_codes[:].bitcast(FP8X4), rhs_scale=tok_plane[:], start=True, stop=True,
+            )
+            neg.append(sb(f"neg{t}", [P, S], F32))
+            pos.append(sb(f"pos{t}", [P, S], F32))
+            nc.scalar.activation(neg[t][:], acc[:], ACT.Copy, scale=gain_neg[:, t : t + 1])
+            nc.scalar.activation(pos[t][:], acc[:], ACT.Copy, scale=gain_pos[:, t : t + 1])
+
+        cand_bytes = gather("cand_bytes", x_bytes, cand_t, U8)
+        cand_picked = gather("cand_picked", x_table, cand_t, U32)
+        cand_plane = deal_bytes("cand_plane", cand_bytes)
+        cand_codes = deal_words("cand_codes", cand_picked)
+
+        s_acc = [psum.tile([P, S], F32, name=f"s_acc{t}") for t in range(PACK)]
+        s_win = [sb(f"s_win{t}", [P, S], F32) for t in range(PACK)]
+        s_neg = [sb(f"s_neg{t}", [P, S], F32) for t in range(PACK)]
+
+        def walk_words(tile):
+            return tile[:].rearrange("p (c i t) -> p c t i", t=PACK, i=2)
+
+        def walk_planes(tile):
+            return tile[:].rearrange("p t (c i) -> p c t i", i=2)
+
+        pa = [sb(f"pa{ci}", [P, PACK, n], F32) for ci, (c0, n) in enumerate(CH1)]
+        pb = [sb(f"pb{ci}", [P, PACK, n], F32) for ci, (c0, n) in enumerate(CH1)]
+        upper = [sb(f"upper{ci}", [P, PACK, n], F32) for ci, (c0, n) in enumerate(CH1)]
+        raised = [sb(f"raised{ci}", [P, PACK, n], F32) for ci, (c0, n) in enumerate(CH1)]
+        z = [sb(f"z{ci}", [P, PACK * n], BF16) for ci, (c0, n) in enumerate(CH1)]
+        s_out = [[s_acc[t][:, 0:256], h_acc[t][:, 0:128], s_acc[t][:, 256:384]] for t in range(PACK)]
+
+        def look_a(ci, t):
+            c0, n = CH1[ci]
+            nc.vector.tensor_tensor(pa[ci][:, t, :], neg[t][:].indirect(entries(n1_t, c0, n)), pos[t][:, c0 : c0 + n], ALU.add)
+            if t == PACK - 1:
+                nc.scalar.activation(upper[ci][:], pa[ci][:], ACT.Relu)
+
+        def look_b(ci, t):
+            c0, n = CH1[ci]
+            nc.vector.tensor_tensor(pb[ci][:, t, :], pos[t][:].indirect(entries(n2_t, c0, n)), neg[t][:, c0 : c0 + n], ALU.add)
+
+        def clamp_low(ci):
+            nc.vector.scalar_tensor_tensor(raised[ci][:], pa[ci][:], 0.0, pb[ci][:], ALU.min, ALU.max)
+
+        def clamp_high(ci):
+            nc.vector.tensor_tensor(walk_words(z[ci]), walk_planes(upper[ci]), walk_planes(raised[ci]), ALU.min)
+
+        def score(ci):
+            c0, n = CH1[ci]
+            z_codes = sb(f"z_codes{ci}", [P, n], U32)
+            z_plane = sb(f"z_plane{ci}", [P, n], U8)
+            nc.vector.quantize_mx(out=z_codes[:].bitcast(FP8X4), scales=z_plane[:], in_=z[ci][:])
+            for t in range(PACK):
+                rows = slice(P * t, P * (t + 1))
+                nc.tensor.matmul_mx(
+                    out=s_out[t][ci], lhsT=cand_codes[:, rows].bitcast(FP8X4), lhsT_scale=cand_plane[:, rows],
+                    rhs=z_codes[:].bitcast(FP8X4), rhs_scale=z_plane[:], start=True, stop=True,
+                )
+                nc.scalar.activation(s_win[t][:, c0 : c0 + n], s_out[t][ci], ACT.Copy, scale=0.75 * 0.0625)
+
+        def negate(ci):
+            c0, n = CH1[ci]
+            for t in range(PACK):
+                nc.scalar.activation(s_neg[t][:, c0 : c0 + n], s_out[t][ci], ACT.Copy, scale=-0.0625)
+
+        for t in range(PACK):
+            look_a(0, t)
+            look_b(0, t)
+        look_a(1, 0)
+        clamp_low(0)
+        look_a(1, 1)
+        clamp_high(0)
+        look_a(1, 2)
+        score(0)
+        negate(0)
+        look_a(1, 3)
+        for t in range(PACK):
+            look_b(1, t)
+        look_a(2, 0)
+        clamp_low(1)
+        look_a(2, 1)
+        clamp_high(1)
+        look_a(2, 2)
+        score(1)
+        look_a(2, 3)
+        for t in range(PACK):
+            look_b(2, t)
+        clamp_low(2)
+        clamp_high(2)
+        score(2)
+        negate(1)
+        negate(2)
+
+        out_rows = out_0.rearrange("(p t) j -> p t j", t=PACK)
+        out_words = out_1[0].rearrange("p n t -> p (n t)").bitcast(I32)
+        y_plane = sb("y_plane", [P, S], U8)
+        for ci, (c0, n) in enumerate(CH2):
+            cols = slice(c0, c0 + n)
+            y = sb(f"y{ci}", [P, PACK, n], F32)
+            part = []
+            for t in range(PACK + 1):
+                if t < PACK:
+                    part.append(sb(f"part{ci}_{t}", [P, n], F32))
+                    nc.vector.tensor_tensor(part[t][:], s_win[t][:].indirect(entries(n3_t, c0, n)), s_neg[t][:, cols], ALU.add)
+                if t > 0:
+                    nc.vector.tensor_tensor(y[:, t - 1, :], s_win[t - 1][:].indirect(entries(n4_t, c0, n)), part[t - 1][:], ALU.add)
+            nc.sync.dma_start(out_rows[:, :, cols], y[:])
+            y_bf = sb(f"y_bf{ci}", [P, PACK * n], BF16)
+            dst = y_bf[:].rearrange("p (c i t) -> p c t i", t=PACK, i=2)
+            src = y[:].rearrange("p t (c i) -> p c t i", i=2)
+            if ci == len(CH2) - 1:
+                nc.vector.tensor_copy(dst, src)
+            else:
+                nc.scalar.copy(dst, src)
+            y_codes = sb(f"y_codes{ci}", [P, n], U32)
+            nc.vector.quantize_mx(out=y_codes[:].bitcast(FP8X4), scales=y_plane[:, cols], in_=y_bf[:])
+            nc.sync.dma_start(out_words[:, cols], y_codes[:].bitcast(I32))
+        for q in range(4):
+            queue = nc.scalar if q % 2 else nc.sync
+            queue.dma_start(out_2[0, 4 * q : 4 * q + 4, :].bitcast(I32), y_plane[32 * q : 32 * q + 4, :].bitcast(I32))

@@ -1,6 +1,7 @@
 from contextlib import ExitStack
 
 import concourse.mybir as mybir
+from concourse.masks import make_identity
 
 K, T, S, G = 512, 1024, 512, 2048
 FLOPS = 2 * 2 * 512 * 512 * 512
@@ -18,6 +19,7 @@ ACT = mybir.ActivationFunctionType
 P = 128
 PACK = 4
 CH1 = [(0, 256), (256, 128), (384, 128)]
+PE_CHUNKS = 1
 CH2 = [(0, 256), (256, 128), (384, 128)]
 
 
@@ -29,8 +31,8 @@ def tile_picked_pqcminmodlap_none_po_kernel(
         keep = ctx.enter_context(tc.tile_pool(name="keep", bufs=1))
         psum = ctx.enter_context(tc.psum_pool(name="psum", bufs=1))
 
-        def sb(name, shape, dtype):
-            return keep.tile(shape, dtype, name=name, align_bytes=64)
+        def sb(name, shape, dtype, tag=None):
+            return keep.tile(shape, dtype, name=name, tag=tag or name, align_bytes=64)
 
         def load_list(name, src):
             tile = sb(name, [P, S // 16], U16)
@@ -59,6 +61,8 @@ def tile_picked_pqcminmodlap_none_po_kernel(
         nc.sync.dma_start(d_table[:].bitcast(I32), d_words[0].rearrange("p n t -> p (n t)").bitcast(I32))
         nc.gpsimd.dma_start(gain[:], gs.rearrange("(p t) o -> p (t o)", t=PACK))
 
+        ident = sb("ident", [P, P], F32)
+        make_identity(nc, ident[:])
         gain_pos = sb("gain_pos", [P, PACK], F32)
         gain_neg = sb("gain_neg", [P, PACK], F32)
         nc.scalar.activation(gain_pos[:], gain[:], ACT.Copy, scale=0.0625)
@@ -133,7 +137,7 @@ def tile_picked_pqcminmodlap_none_po_kernel(
         upper = [sb(f"upper{ci}", [P, PACK, n], F32) for ci, (c0, n) in enumerate(CH1)]
         raised = [sb(f"raised{ci}", [P, PACK, n], F32) for ci, (c0, n) in enumerate(CH1)]
         z = [sb(f"z{ci}", [P, PACK * n], BF16) for ci, (c0, n) in enumerate(CH1)]
-        s_out = [[s_acc[t][:, 0:256], h_acc[t][:, 0:128], s_acc[t][:, 256:384]] for t in range(PACK)]
+        s_out = [[s_acc[t][:, 0:256], h_acc[t][:, 0:128], h_acc[t][:, 128:256]] for t in range(PACK)]
 
         def look_a(ci, t):
             c0, n = CH1[ci]
@@ -194,24 +198,42 @@ def tile_picked_pqcminmodlap_none_po_kernel(
         clamp_low(2)
         clamp_high(2)
         score(2)
-        negate(1)
-        negate(2)
+        for t in range(PACK):
+            nc.scalar.activation(s_neg[t][:, 256:512], h_acc[t][:, 0:256], ACT.Copy, scale=-0.0625)
 
         out_rows = out_0.rearrange("(p t) j -> p t j", t=PACK)
         out_words = out_1[0].rearrange("p n t -> p (n t)").bitcast(I32)
         y_plane = sb("y_plane", [P, S], U8)
         for ci, (c0, n) in enumerate(CH2):
             cols = slice(c0, c0 + n)
-            y = sb(f"y{ci}", [P, PACK, n], F32)
+            y = sb(f"y{ci}", [P, PACK, n], F32, tag="y_bf0" if ci == 2 else None)
             part = []
-            for t in range(PACK + 1):
+            if ci < PE_CHUNKS:
+                turned = []
+                for t in range(PACK + 1):
+                    if t < PACK:
+                        g3 = sb(f"g3_{ci}_{t}", [P, n], F32)
+                        g4 = sb(f"g4_{ci}_{t}", [P, n], F32)
+                        nc.vector.tensor_copy(g3[:], s_win[t][:].indirect(entries(n3_t, c0, n)))
+                        nc.vector.tensor_copy(g4[:], s_win[t][:].indirect(entries(n4_t, c0, n)))
+                        for b in range(0, n, P):
+                            terms = [s_neg[t][:, c0 + b : c0 + b + P], g3[:, b : b + P], g4[:, b : b + P]]
+                            for i, term in enumerate(terms):
+                                nc.tensor.matmul(s_acc[t][:, b : b + P], term, ident[:], is_transpose=True, start=i == 0, stop=i == 2)
+                        turned.append(sb(f"turned{ci}_{t}", [P, n], F32))
+                        nc.scalar.copy(turned[t][:], s_acc[t][:, 0:n])
+                    if t > 0:
+                        for b in range(0, n, P):
+                            nc.tensor.transpose(s_acc[t - 1][:, n + b : n + b + P], turned[t - 1][:, b : b + P], ident[:])
+                        nc.scalar.copy(y[:, t - 1, :], s_acc[t - 1][:, n : 2 * n])
+            for t in range(PACK + 1 if ci >= PE_CHUNKS else 0):
                 if t < PACK:
                     part.append(sb(f"part{ci}_{t}", [P, n], F32))
                     nc.vector.tensor_tensor(part[t][:], s_win[t][:].indirect(entries(n3_t, c0, n)), s_neg[t][:, cols], ALU.add)
                 if t > 0:
                     nc.vector.tensor_tensor(y[:, t - 1, :], s_win[t - 1][:].indirect(entries(n4_t, c0, n)), part[t - 1][:], ALU.add)
             nc.sync.dma_start(out_rows[:, :, cols], y[:])
-            y_bf = sb(f"y_bf{ci}", [P, PACK * n], BF16)
+            y_bf = sb(f"y_bf{ci}", [P, PACK * n], BF16, tag="turned0_3" if ci == 1 else None)
             dst = y_bf[:].rearrange("p (c i t) -> p c t i", t=PACK, i=2)
             src = y[:].rearrange("p t (c i) -> p c t i", i=2)
             if ci == len(CH2) - 1:

@@ -1,7 +1,6 @@
 from contextlib import ExitStack
 
 import concourse.mybir as mybir
-from concourse.masks import make_identity
 
 K, T, S, G = 512, 1024, 512, 2048
 FLOPS = 2 * 2 * 512 * 512 * 512
@@ -18,9 +17,8 @@ ACT = mybir.ActivationFunctionType
 
 P = 128
 PACK = 4
-CH1 = [(0, 256), (256, 128), (384, 128)]
-PE_CHUNKS = 1
-CH2 = [(0, 256), (256, 128), (384, 128)]
+HALF = S // 2
+PIECES = [(0, 256), (256, 128), (384, 128)]
 
 
 def tile_picked_pqcminmodlap_none_po_kernel(
@@ -31,8 +29,8 @@ def tile_picked_pqcminmodlap_none_po_kernel(
         keep = ctx.enter_context(tc.tile_pool(name="keep", bufs=1))
         psum = ctx.enter_context(tc.psum_pool(name="psum", bufs=1))
 
-        def sb(name, shape, dtype, tag=None):
-            return keep.tile(shape, dtype, name=name, tag=tag or name, align_bytes=64)
+        def sb(name, shape, dtype):
+            return keep.tile(shape, dtype, name=name, align_bytes=64)
 
         def load_list(name, src):
             tile = sb(name, [P, S // 16], U16)
@@ -41,32 +39,6 @@ def tile_picked_pqcminmodlap_none_po_kernel(
 
         def entries(tile, start, count):
             return tile[:, start // 16 : (start + count) // 16]
-
-        d_bytes = sb("d_bytes", [P, G], U8)
-        x_bytes = sb("x_bytes", [P, T], U8)
-        d_plane = sb("d_plane", [P, S], U8)
-        x_table = sb("x_table", [P, T], U32)
-        d_table = sb("d_table", [P, G], U32)
-        gain = sb("gain", [P, PACK], F32)
-        nc.vector.memset(d_bytes[:].bitcast(I32), 0)
-        nc.gpsimd.memset(x_bytes[:].bitcast(I32), 0)
-        nc.gpsimd.memset(d_plane[:].bitcast(I32), 0)
-
-        k1_t = load_list("k1_t", k1)
-        nc.sync.dma_start(d_bytes[0:P:8, :].bitcast(I32), d_scales[0].bitcast(I32))
-        offs_t = load_list("offs_t", offs)
-        for q in range(4):
-            nc.sync.dma_start(x_bytes[32 * q : 32 * q + 4, :].bitcast(I32), x_scales[0, 4 * q : 4 * q + 4, :].bitcast(I32))
-        nc.sync.dma_start(x_table[:].bitcast(I32), x_words[0].rearrange("p n t -> p (n t)").bitcast(I32))
-        nc.sync.dma_start(d_table[:].bitcast(I32), d_words[0].rearrange("p n t -> p (n t)").bitcast(I32))
-        nc.gpsimd.dma_start(gain[:], gs.rearrange("(p t) o -> p (t o)", t=PACK))
-
-        ident = sb("ident", [P, P], F32)
-        make_identity(nc, ident[:])
-        gain_pos = sb("gain_pos", [P, PACK], F32)
-        gain_neg = sb("gain_neg", [P, PACK], F32)
-        nc.scalar.activation(gain_pos[:], gain[:], ACT.Copy, scale=0.0625)
-        nc.scalar.activation(gain_neg[:], gain[:], ACT.Copy, scale=-0.0625)
 
         def gather(name, table, lst, dtype):
             picked = sb(name, [P, S], dtype)
@@ -89,89 +61,116 @@ def tile_picked_pqcminmodlap_none_po_kernel(
             )
             return dealt
 
+        def as_words(ap):
+            return ap.rearrange("p (c i t) -> p c t i", t=PACK, i=2)
+
+        def as_planes(ap):
+            return ap.rearrange("p t (c i) -> p c t i", i=2)
+
+        d_bytes = sb("d_bytes", [P, G], U8)
+        x_bytes = sb("x_bytes", [P, T], U8)
+        d_plane = sb("d_plane", [P, S], U8)
+        x_table = sb("x_table", [P, T], U32)
+        d_table = sb("d_table", [P, G], U32)
+        gain = sb("gain", [P, PACK], F32)
+        nc.gpsimd.memset(d_bytes[:].bitcast(I32), 0)
+        nc.vector.memset(x_bytes[:].bitcast(I32), 0)
+        nc.vector.memset(d_plane[:].bitcast(I32), 0)
+
+        k1_t = load_list("k1_t", k1)
+        nc.sync.dma_start(d_bytes[0:P:8, :].bitcast(I32), d_scales[0].bitcast(I32))
+        for q in range(4):
+            nc.scalar.dma_start(x_bytes[32 * q : 32 * q + 4, :].bitcast(I32), x_scales[0, 4 * q : 4 * q + 4, :].bitcast(I32))
+        offs_t = load_list("offs_t", offs)
+        nc.sync.dma_start(x_table[:].bitcast(I32), x_words[0].rearrange("p n t -> p (n t)").bitcast(I32))
+        nc.sync.dma_start(d_table[:].bitcast(I32), d_words[0].rearrange("p n t -> p (n t)").bitcast(I32))
+
         d_bytes_picked = gather("d_bytes_picked", d_bytes, k1_t, U8)
         d_bytes_dealt = deal_bytes("d_bytes_dealt", d_bytes_picked)
         for j in range(4):
-            nc.sync.dma_start(d_plane[j:P:32, :].bitcast(I32), d_bytes_dealt[8 * j : P : 32, :].bitcast(I32))
+            queue = nc.scalar if j % 2 else nc.sync
+            queue.dma_start(d_plane[j:P:32, :].bitcast(I32), d_bytes_dealt[8 * j : P : 32, :].bitcast(I32))
         cand_t = load_list("cand_t", cand)
+        nc.sync.dma_start(gain[:], gs.rearrange("(p t) o -> p (t o)", t=PACK))
         n1_t = load_list("n1_t", n1)
         n2_t = load_list("n2_t", n2)
         n3_t = load_list("n3_t", n3)
         n4_t = load_list("n4_t", n4)
+        gain_pos = sb("gain_pos", [P, PACK], F32)
+        gain_neg = sb("gain_neg", [P, PACK], F32)
+        nc.scalar.activation(gain_pos[:], gain[:], ACT.Copy, scale=0.0625)
+        nc.scalar.activation(gain_neg[:], gain[:], ACT.Copy, scale=-0.0625)
+
         tok_plane = gather("tok_plane", x_bytes, offs_t, U8)
         tok_codes = gather("tok_codes", x_table, offs_t, U32)
         d_picked = gather("d_picked", d_table, k1_t, U32)
         d_codes = deal_words("d_codes", d_picked)
 
-        pos, neg, h_acc = [], [], []
+        h_acc = [psum.tile([P, S], F32, name=f"h_acc{t}") for t in range(PACK)]
+        s_acc = [psum.tile([P, S], F32, name=f"s_acc{t}") for t in range(PACK)]
+        pos = [sb(f"pos{t}", [P, S], F32) for t in range(PACK)]
+        neg = [sb(f"neg{t}", [P, S], F32) for t in range(PACK)]
         for t in range(PACK):
-            cols = slice(P * t, P * (t + 1))
-            acc = psum.tile([P, S], F32, name=f"h_acc{t}")
-            h_acc.append(acc)
+            rows = slice(P * t, P * (t + 1))
             nc.tensor.matmul_mx(
-                out=acc[:], lhsT=d_codes[:, cols].bitcast(FP8X4), lhsT_scale=d_plane[:, cols],
+                out=h_acc[t][:], lhsT=d_codes[:, rows].bitcast(FP8X4), lhsT_scale=d_plane[:, rows],
                 rhs=tok_codes[:].bitcast(FP8X4), rhs_scale=tok_plane[:], start=True, stop=True,
             )
-            neg.append(sb(f"neg{t}", [P, S], F32))
-            pos.append(sb(f"pos{t}", [P, S], F32))
-            nc.scalar.activation(neg[t][:], acc[:], ACT.Copy, scale=gain_neg[:, t : t + 1])
-            nc.scalar.activation(pos[t][:], acc[:], ACT.Copy, scale=gain_pos[:, t : t + 1])
+            nc.scalar.activation(neg[t][:], h_acc[t][:], ACT.Copy, scale=gain_neg[:, t : t + 1])
+            nc.scalar.activation(pos[t][:], h_acc[t][:], ACT.Copy, scale=gain_pos[:, t : t + 1])
 
         cand_bytes = gather("cand_bytes", x_bytes, cand_t, U8)
         cand_picked = gather("cand_picked", x_table, cand_t, U32)
         cand_plane = deal_bytes("cand_plane", cand_bytes)
         cand_codes = deal_words("cand_codes", cand_picked)
 
-        s_acc = [psum.tile([P, S], F32, name=f"s_acc{t}") for t in range(PACK)]
         s_win = [sb(f"s_win{t}", [P, S], F32) for t in range(PACK)]
         s_neg = [sb(f"s_neg{t}", [P, S], F32) for t in range(PACK)]
+        pa = [sb(f"pa{h}", [P, PACK, HALF], F32) for h in range(2)]
+        pb = [sb(f"pb{h}", [P, PACK, HALF], F32) for h in range(2)]
+        upper = [sb(f"upper{h}", [P, PACK, HALF], F32) for h in range(2)]
+        raised = [sb(f"raised{i}", [P, PACK, n], F32) for i, (c0, n) in enumerate(PIECES)]
+        z = [sb(f"z{i}", [P, PACK * n], BF16) for i, (c0, n) in enumerate(PIECES)]
+        z_codes = sb("z_codes", [P, S], U32)
+        z_plane = sb("z_plane", [P, S], U8)
 
-        def walk_words(tile):
-            return tile[:].rearrange("p (c i t) -> p c t i", t=PACK, i=2)
-
-        def walk_planes(tile):
-            return tile[:].rearrange("p t (c i) -> p c t i", i=2)
-
-        pa = [sb(f"pa{ci}", [P, PACK, n], F32) for ci, (c0, n) in enumerate(CH1)]
-        pb = [sb(f"pb{ci}", [P, PACK, n], F32) for ci, (c0, n) in enumerate(CH1)]
-        upper = [sb(f"upper{ci}", [P, PACK, n], F32) for ci, (c0, n) in enumerate(CH1)]
-        raised = [sb(f"raised{ci}", [P, PACK, n], F32) for ci, (c0, n) in enumerate(CH1)]
-        z = [sb(f"z{ci}", [P, PACK * n], BF16) for ci, (c0, n) in enumerate(CH1)]
-        s_out = [[s_acc[t][:, 0:256], h_acc[t][:, 0:128], h_acc[t][:, 128:256]] for t in range(PACK)]
-
-        def look_a(ci, t):
-            c0, n = CH1[ci]
-            nc.vector.tensor_tensor(pa[ci][:, t, :], neg[t][:].indirect(entries(n1_t, c0, n)), pos[t][:, c0 : c0 + n], ALU.add)
+        def look_a(h, t):
+            nc.vector.tensor_tensor(
+                pa[h][:, t, :], neg[t][:].indirect(entries(n1_t, h * HALF, HALF)), pos[t][:, h * HALF : (h + 1) * HALF], ALU.add
+            )
             if t == PACK - 1:
-                nc.scalar.activation(upper[ci][:], pa[ci][:], ACT.Relu)
+                nc.scalar.activation(upper[h][:], pa[h][:], ACT.Relu)
 
-        def look_b(ci, t):
-            c0, n = CH1[ci]
-            nc.vector.tensor_tensor(pb[ci][:, t, :], pos[t][:].indirect(entries(n2_t, c0, n)), neg[t][:, c0 : c0 + n], ALU.add)
+        def look_b(h, t):
+            nc.vector.tensor_tensor(
+                pb[h][:, t, :], pos[t][:].indirect(entries(n2_t, h * HALF, HALF)), neg[t][:, h * HALF : (h + 1) * HALF], ALU.add
+            )
 
-        def clamp_low(ci):
-            nc.vector.scalar_tensor_tensor(raised[ci][:], pa[ci][:], 0.0, pb[ci][:], ALU.min, ALU.max)
+        def piece_of(tiles, i):
+            c0, n = PIECES[i]
+            return tiles[c0 // HALF][:, :, c0 % HALF : c0 % HALF + n]
 
-        def clamp_high(ci):
-            nc.vector.tensor_tensor(walk_words(z[ci]), walk_planes(upper[ci]), walk_planes(raised[ci]), ALU.min)
+        def clamp_low(i):
+            nc.vector.scalar_tensor_tensor(raised[i][:], piece_of(pa, i), 0.0, piece_of(pb, i), ALU.min, ALU.max)
 
-        def score(ci):
-            c0, n = CH1[ci]
-            z_codes = sb(f"z_codes{ci}", [P, n], U32)
-            z_plane = sb(f"z_plane{ci}", [P, n], U8)
-            nc.vector.quantize_mx(out=z_codes[:].bitcast(FP8X4), scales=z_plane[:], in_=z[ci][:])
+        def clamp_high(i):
+            nc.vector.tensor_tensor(as_words(z[i][:]), as_planes(piece_of(upper, i)), as_planes(raised[i][:]), ALU.min)
+
+        def quantise(i):
+            c0, n = PIECES[i]
+            nc.vector.quantize_mx(out=z_codes[:, c0 : c0 + n].bitcast(FP8X4), scales=z_plane[:, c0 : c0 + n], in_=z[i][:])
+
+        def score(h):
+            cols = slice(h * HALF, (h + 1) * HALF)
             for t in range(PACK):
                 rows = slice(P * t, P * (t + 1))
                 nc.tensor.matmul_mx(
-                    out=s_out[t][ci], lhsT=cand_codes[:, rows].bitcast(FP8X4), lhsT_scale=cand_plane[:, rows],
-                    rhs=z_codes[:].bitcast(FP8X4), rhs_scale=z_plane[:], start=True, stop=True,
+                    out=s_acc[t][:, cols], lhsT=cand_codes[:, rows].bitcast(FP8X4), lhsT_scale=cand_plane[:, rows],
+                    rhs=z_codes[:, cols].bitcast(FP8X4), rhs_scale=z_plane[:, cols], start=True, stop=True,
                 )
-                nc.scalar.activation(s_win[t][:, c0 : c0 + n], s_out[t][ci], ACT.Copy, scale=0.75 * 0.0625)
-
-        def negate(ci):
-            c0, n = CH1[ci]
+                nc.scalar.activation(s_win[t][:, cols], s_acc[t][:, cols], ACT.Copy, scale=0.75 * 0.0625)
             for t in range(PACK):
-                nc.scalar.activation(s_neg[t][:, c0 : c0 + n], s_out[t][ci], ACT.Copy, scale=-0.0625)
+                nc.scalar.activation(s_neg[t][:, cols], s_acc[t][:, cols], ACT.Copy, scale=-0.0625)
 
         for t in range(PACK):
             look_a(0, t)
@@ -181,68 +180,61 @@ def tile_picked_pqcminmodlap_none_po_kernel(
         look_a(1, 1)
         clamp_high(0)
         look_a(1, 2)
+        quantise(0)
         score(0)
-        negate(0)
         look_a(1, 3)
         for t in range(PACK):
             look_b(1, t)
-        look_a(2, 0)
         clamp_low(1)
-        look_a(2, 1)
-        clamp_high(1)
-        look_a(2, 2)
-        score(1)
-        look_a(2, 3)
-        for t in range(PACK):
-            look_b(2, t)
         clamp_low(2)
+        clamp_high(1)
         clamp_high(2)
-        score(2)
-        for t in range(PACK):
-            nc.scalar.activation(s_neg[t][:, 256:512], h_acc[t][:, 0:256], ACT.Copy, scale=-0.0625)
+        quantise(1)
+        quantise(2)
+        score(1)
 
         out_rows = out_0.rearrange("(p t) j -> p t j", t=PACK)
         out_words = out_1[0].rearrange("p n t -> p (n t)").bitcast(I32)
         y_plane = sb("y_plane", [P, S], U8)
-        for ci, (c0, n) in enumerate(CH2):
+        part = [[sb(f"part{h}_{t}", [P, HALF], F32) for t in range(PACK)] for h in range(2)]
+        y = [sb(f"y{i}", [P, PACK, n], F32) for i, (c0, n) in enumerate(PIECES)]
+
+        def look_3(h, t):
+            nc.vector.tensor_tensor(
+                part[h][t][:], s_win[t][:].indirect(entries(n3_t, h * HALF, HALF)), s_neg[t][:, h * HALF : (h + 1) * HALF], ALU.add
+            )
+
+        def look_4(i, t):
+            c0, n = PIECES[i]
+            nc.vector.tensor_tensor(
+                y[i][:, t, :], s_win[t][:].indirect(entries(n4_t, c0, n)), part[c0 // HALF][t][:, c0 % HALF : c0 % HALF + n], ALU.add
+            )
+
+        def hand_out(i):
+            c0, n = PIECES[i]
             cols = slice(c0, c0 + n)
-            y = sb(f"y{ci}", [P, PACK, n], F32, tag="y_bf0" if ci == 2 else None)
-            part = []
-            if ci < PE_CHUNKS:
-                turned = []
-                for t in range(PACK + 1):
-                    if t < PACK:
-                        g3 = sb(f"g3_{ci}_{t}", [P, n], F32)
-                        g4 = sb(f"g4_{ci}_{t}", [P, n], F32)
-                        nc.vector.tensor_copy(g3[:], s_win[t][:].indirect(entries(n3_t, c0, n)))
-                        nc.vector.tensor_copy(g4[:], s_win[t][:].indirect(entries(n4_t, c0, n)))
-                        for b in range(0, n, P):
-                            terms = [s_neg[t][:, c0 + b : c0 + b + P], g3[:, b : b + P], g4[:, b : b + P]]
-                            for i, term in enumerate(terms):
-                                nc.tensor.matmul(s_acc[t][:, b : b + P], term, ident[:], is_transpose=True, start=i == 0, stop=i == 2)
-                        turned.append(sb(f"turned{ci}_{t}", [P, n], F32))
-                        nc.scalar.copy(turned[t][:], s_acc[t][:, 0:n])
-                    if t > 0:
-                        for b in range(0, n, P):
-                            nc.tensor.transpose(s_acc[t - 1][:, n + b : n + b + P], turned[t - 1][:, b : b + P], ident[:])
-                        nc.scalar.copy(y[:, t - 1, :], s_acc[t - 1][:, n : 2 * n])
-            for t in range(PACK + 1 if ci >= PE_CHUNKS else 0):
-                if t < PACK:
-                    part.append(sb(f"part{ci}_{t}", [P, n], F32))
-                    nc.vector.tensor_tensor(part[t][:], s_win[t][:].indirect(entries(n3_t, c0, n)), s_neg[t][:, cols], ALU.add)
-                if t > 0:
-                    nc.vector.tensor_tensor(y[:, t - 1, :], s_win[t - 1][:].indirect(entries(n4_t, c0, n)), part[t - 1][:], ALU.add)
-            nc.sync.dma_start(out_rows[:, :, cols], y[:])
-            y_bf = sb(f"y_bf{ci}", [P, PACK * n], BF16, tag="turned0_3" if ci == 1 else None)
-            dst = y_bf[:].rearrange("p (c i t) -> p c t i", t=PACK, i=2)
-            src = y[:].rearrange("p t (c i) -> p c t i", i=2)
-            if ci == len(CH2) - 1:
-                nc.vector.tensor_copy(dst, src)
+            nc.sync.dma_start(out_rows[:, :, cols], y[i][:])
+            y_bf = sb(f"y_bf{i}", [P, PACK * n], BF16)
+            if i == len(PIECES) - 1:
+                nc.vector.tensor_copy(as_words(y_bf[:]), as_planes(y[i][:]))
             else:
-                nc.scalar.copy(dst, src)
-            y_codes = sb(f"y_codes{ci}", [P, n], U32)
+                nc.scalar.copy(as_words(y_bf[:]), as_planes(y[i][:]))
+            y_codes = sb(f"y_codes{i}", [P, n], U32)
             nc.vector.quantize_mx(out=y_codes[:].bitcast(FP8X4), scales=y_plane[:, cols], in_=y_bf[:])
             nc.sync.dma_start(out_words[:, cols], y_codes[:].bitcast(I32))
+
+        look_3(0, 0)
+        for t in range(PACK):
+            if t + 1 < PACK:
+                look_3(0, t + 1)
+            look_4(0, t)
+        hand_out(0)
+        for t in range(PACK):
+            look_3(1, t)
+        for i in (1, 2):
+            for t in range(PACK):
+                look_4(i, t)
+            hand_out(i)
         for q in range(4):
             queue = nc.scalar if q % 2 else nc.sync
             queue.dma_start(out_2[0, 4 * q : 4 * q + 4, :].bitcast(I32), y_plane[32 * q : 32 * q + 4, :].bitcast(I32))

from contextlib import ExitStack

import concourse.mybir as mybir

K, T, S, G = 512, 1024, 512, 2048
FLOPS = 2 * 2 * 512 * 512 * 512

F32 = mybir.dt.float32
BF16 = mybir.dt.bfloat16
I32 = mybir.dt.int32
U32 = mybir.dt.uint32
U16 = mybir.dt.uint16
U8 = mybir.dt.uint8
FP8X4 = mybir.dt.float8_e4m3fn_x4
ALU = mybir.AluOpType
ACT = mybir.ActivationFunctionType

P = 128
PACK = 4
HALF = S // 2
PIECES = [(0, 256), (256, 128), (384, 128)]


def tile_picked_pqcminmodlap_none_po_kernel(
    tc, x_words, x_scales, d_words, d_scales, gs, offs, k1, n1, n2, cand, n3, n4, out_0, out_1, out_2
):
    nc = tc.nc
    with ExitStack() as ctx:
        keep = ctx.enter_context(tc.tile_pool(name="keep", bufs=1))
        psum = ctx.enter_context(tc.psum_pool(name="psum", bufs=1))

        def sb(name, shape, dtype):
            return keep.tile(shape, dtype, name=name, align_bytes=64)

        def load_list(name, src):
            tile = sb(name, [P, S // 16], U16)
            nc.sync.dma_start(tile[:], src)
            return tile

        def entries(tile, start, count):
            return tile[:, start // 16 : (start + count) // 16]

        def gather(name, table, lst, dtype):
            picked = sb(name, [P, S], dtype)
            nc.vector.tensor_copy(picked[:], table[:].indirect(lst[:]))
            return picked

        def deal_words(name, picked):
            dealt = sb(name, [P, S], U32)
            nc.vector.tensor_copy(
                dealt[:].rearrange("p (t c i) -> p c t i", t=PACK, i=4),
                picked[:].rearrange("p (c i t) -> p c t i", t=PACK, i=4),
            )
            return dealt

        def deal_bytes(name, picked):
            dealt = sb(name, [P, S], U8)
            nc.vector.tensor_copy(
                dealt[:].rearrange("p (t m) -> p t m", t=PACK),
                picked[:].rearrange("p (m t) -> p t m", t=PACK),
            )
            return dealt

        def as_words(ap):
            return ap.rearrange("p (c i t) -> p c t i", t=PACK, i=2)

        def as_planes(ap):
            return ap.rearrange("p t (c i) -> p c t i", i=2)

        d_bytes = sb("d_bytes", [P, G], U8)
        x_bytes = sb("x_bytes", [P, T], U8)
        d_plane = sb("d_plane", [P, S], U8)
        x_table = sb("x_table", [P, T], U32)
        d_table = sb("d_table", [P, G], U32)
        gain = sb("gain", [P, PACK], F32)
        nc.gpsimd.memset(d_bytes[:].bitcast(I32), 0)
        nc.vector.memset(x_bytes[:].bitcast(I32), 0)
        nc.vector.memset(d_plane[:].bitcast(I32), 0)

        k1_t = load_list("k1_t", k1)
        nc.sync.dma_start(d_bytes[0:P:8, :].bitcast(I32), d_scales[0].bitcast(I32))
        for q in range(4):
            nc.scalar.dma_start(x_bytes[32 * q : 32 * q + 4, :].bitcast(I32), x_scales[0, 4 * q : 4 * q + 4, :].bitcast(I32))
        offs_t = load_list("offs_t", offs)
        nc.sync.dma_start(x_table[:].bitcast(I32), x_words[0].rearrange("p n t -> p (n t)").bitcast(I32))
        nc.sync.dma_start(d_table[:].bitcast(I32), d_words[0].rearrange("p n t -> p (n t)").bitcast(I32))

        d_bytes_picked = gather("d_bytes_picked", d_bytes, k1_t, U8)
        d_bytes_dealt = deal_bytes("d_bytes_dealt", d_bytes_picked)
        for j in range(4):
            queue = nc.scalar if j % 2 else nc.sync
            queue.dma_start(d_plane[j:P:32, :].bitcast(I32), d_bytes_dealt[8 * j : P : 32, :].bitcast(I32))
        cand_t = load_list("cand_t", cand)
        nc.sync.dma_start(gain[:], gs.rearrange("(p t) o -> p (t o)", t=PACK))
        n1_t = load_list("n1_t", n1)
        n2_t = load_list("n2_t", n2)
        n3_t = load_list("n3_t", n3)
        n4_t = load_list("n4_t", n4)
        gain_pos = sb("gain_pos", [P, PACK], F32)
        gain_neg = sb("gain_neg", [P, PACK], F32)
        nc.scalar.activation(gain_pos[:], gain[:], ACT.Copy, scale=0.0625)
        nc.scalar.activation(gain_neg[:], gain[:], ACT.Copy, scale=-0.0625)

        tok_plane = gather("tok_plane", x_bytes, offs_t, U8)
        tok_codes = gather("tok_codes", x_table, offs_t, U32)
        d_picked = gather("d_picked", d_table, k1_t, U32)
        d_codes = deal_words("d_codes", d_picked)

        h_acc = [psum.tile([P, S], F32, name=f"h_acc{t}") for t in range(PACK)]
        s_acc = [psum.tile([P, S], F32, name=f"s_acc{t}") for t in range(PACK)]
        pos = [sb(f"pos{t}", [P, S], F32) for t in range(PACK)]
        neg = [sb(f"neg{t}", [P, S], F32) for t in range(PACK)]
        for t in range(PACK):
            rows = slice(P * t, P * (t + 1))
            nc.tensor.matmul_mx(
                out=h_acc[t][:], lhsT=d_codes[:, rows].bitcast(FP8X4), lhsT_scale=d_plane[:, rows],
                rhs=tok_codes[:].bitcast(FP8X4), rhs_scale=tok_plane[:], start=True, stop=True,
            )
            nc.scalar.activation(neg[t][:], h_acc[t][:], ACT.Copy, scale=gain_neg[:, t : t + 1])
            nc.scalar.activation(pos[t][:], h_acc[t][:], ACT.Copy, scale=gain_pos[:, t : t + 1])

        cand_bytes = gather("cand_bytes", x_bytes, cand_t, U8)
        cand_picked = gather("cand_picked", x_table, cand_t, U32)
        cand_plane = deal_bytes("cand_plane", cand_bytes)
        cand_codes = deal_words("cand_codes", cand_picked)

        s_win = [sb(f"s_win{t}", [P, S], F32) for t in range(PACK)]
        s_neg = [sb(f"s_neg{t}", [P, S], F32) for t in range(PACK)]
        pa = [sb(f"pa{h}", [P, PACK, HALF], F32) for h in range(2)]
        pb = [sb(f"pb{h}", [P, PACK, HALF], F32) for h in range(2)]
        upper = [sb(f"upper{h}", [P, PACK, HALF], F32) for h in range(2)]
        raised = [sb(f"raised{i}", [P, PACK, n], F32) for i, (c0, n) in enumerate(PIECES)]
        z = [sb(f"z{i}", [P, PACK * n], BF16) for i, (c0, n) in enumerate(PIECES)]
        z_codes = sb("z_codes", [P, S], U32)
        z_plane = sb("z_plane", [P, S], U8)

        def look_a(h, t):
            nc.vector.tensor_tensor(
                pa[h][:, t, :], neg[t][:].indirect(entries(n1_t, h * HALF, HALF)), pos[t][:, h * HALF : (h + 1) * HALF], ALU.add
            )
            if t == PACK - 1:
                nc.scalar.activation(upper[h][:], pa[h][:], ACT.Relu)

        def look_b(h, t):
            nc.vector.tensor_tensor(
                pb[h][:, t, :], pos[t][:].indirect(entries(n2_t, h * HALF, HALF)), neg[t][:, h * HALF : (h + 1) * HALF], ALU.add
            )

        def piece_of(tiles, i):
            c0, n = PIECES[i]
            return tiles[c0 // HALF][:, :, c0 % HALF : c0 % HALF + n]

        def clamp_low(i):
            nc.vector.scalar_tensor_tensor(raised[i][:], piece_of(pa, i), 0.0, piece_of(pb, i), ALU.min, ALU.max)

        def clamp_high(i):
            nc.vector.tensor_tensor(as_words(z[i][:]), as_planes(piece_of(upper, i)), as_planes(raised[i][:]), ALU.min)

        def quantise(i):
            c0, n = PIECES[i]
            nc.vector.quantize_mx(out=z_codes[:, c0 : c0 + n].bitcast(FP8X4), scales=z_plane[:, c0 : c0 + n], in_=z[i][:])

        def score(h):
            cols = slice(h * HALF, (h + 1) * HALF)
            for t in range(PACK):
                rows = slice(P * t, P * (t + 1))
                nc.tensor.matmul_mx(
                    out=s_acc[t][:, cols], lhsT=cand_codes[:, rows].bitcast(FP8X4), lhsT_scale=cand_plane[:, rows],
                    rhs=z_codes[:, cols].bitcast(FP8X4), rhs_scale=z_plane[:, cols], start=True, stop=True,
                )
                nc.scalar.activation(s_win[t][:, cols], s_acc[t][:, cols], ACT.Copy, scale=0.75 * 0.0625)
            for t in range(PACK):
                nc.scalar.activation(s_neg[t][:, cols], s_acc[t][:, cols], ACT.Copy, scale=-0.0625)

        for t in range(PACK):
            look_a(0, t)
            look_b(0, t)
        look_a(1, 0)
        clamp_low(0)
        look_a(1, 1)
        clamp_high(0)
        look_a(1, 2)
        quantise(0)
        score(0)
        look_a(1, 3)
        for t in range(PACK):
            look_b(1, t)
        clamp_low(1)
        clamp_low(2)
        clamp_high(1)
        clamp_high(2)
        quantise(1)
        quantise(2)
        score(1)

        out_rows = out_0.rearrange("(p t) j -> p t j", t=PACK)
        out_words = out_1[0].rearrange("p n t -> p (n t)").bitcast(I32)
        y_plane = sb("y_plane", [P, S], U8)
        part = [[sb(f"part{h}_{t}", [P, HALF], F32) for t in range(PACK)] for h in range(2)]
        y = [sb(f"y{i}", [P, PACK, n], F32) for i, (c0, n) in enumerate(PIECES)]

        def look_3(h, t):
            nc.vector.tensor_tensor(
                part[h][t][:], s_win[t][:].indirect(entries(n3_t, h * HALF, HALF)), s_neg[t][:, h * HALF : (h + 1) * HALF], ALU.add
            )

        def look_4(i, t):
            c0, n = PIECES[i]
            nc.vector.tensor_tensor(
                y[i][:, t, :], s_win[t][:].indirect(entries(n4_t, c0, n)), part[c0 // HALF][t][:, c0 % HALF : c0 % HALF + n], ALU.add
            )

        def hand_out(i):
            c0, n = PIECES[i]
            cols = slice(c0, c0 + n)
            nc.sync.dma_start(out_rows[:, :, cols], y[i][:])
            y_bf = sb(f"y_bf{i}", [P, PACK * n], BF16)
            if i == len(PIECES) - 1:
                nc.vector.tensor_copy(as_words(y_bf[:]), as_planes(y[i][:]))
            else:
                nc.scalar.copy(as_words(y_bf[:]), as_planes(y[i][:]))
            y_codes = sb(f"y_codes{i}", [P, n], U32)
            nc.vector.quantize_mx(out=y_codes[:].bitcast(FP8X4), scales=y_plane[:, cols], in_=y_bf[:])
            nc.sync.dma_start(out_words[:, cols], y_codes[:].bitcast(I32))

        look_3(0, 0)
        for t in range(PACK):
            if t + 1 < PACK:
                look_3(0, t + 1)
            look_4(0, t)
        hand_out(0)
        for t in range(PACK):
            look_3(1, t)
        for i in (1, 2):
            for t in range(PACK):
                look_4(i, t)
            hand_out(i)
        for q in range(4):
            queue = nc.scalar if q % 2 else nc.sync
            queue.dma_start(out_2[0, 4 * q : 4 * q + 4, :].bitcast(I32), y_plane[32 * q : 32 * q + 4, :].bitcast(I32))
